import numpy as np
import ml_dtypes


def mxq(x, axis, fmt="e4m3"):
    dtype, down = {"e4m3": (ml_dtypes.float8_e4m3fn, 7), "e5m2": (ml_dtypes.float8_e5m2, 14)}[fmt]
    v = np.moveaxis(np.asarray(x, np.float32).astype(ml_dtypes.bfloat16).astype(np.float64), axis, -1)
    blocks = v.reshape(v.shape[:-1] + (-1, 32))
    amax = np.abs(blocks).max(-1, keepdims=True)
    byte = np.maximum(np.where(amax > 0, np.frexp(amax)[1] - 1 + 127, 0) - down, 1)
    scale = np.exp2(byte - 127.0)
    codes = (blocks / scale).astype(np.float32).astype(dtype).astype(np.float64)
    return np.moveaxis((codes * scale).reshape(v.shape), -1, axis)


WIDE = False


def mx_kscale(k):
    if not WIDE:
        return np.ones(k)
    levels = np.array([10, -10, 5, -5, 0])
    if k % 512:
        return np.exp2(np.random.permutation(np.resize(levels, k // 32))).repeat(32)
    a = np.empty((k // 512, 16))
    for p in range(k // 512):
        a[p, :8] = np.random.permutation(np.resize(levels, 8))
        for g in range(8):
            far = levels[np.abs(levels - a[p, g]) >= 10]
            a[p, g + 8] = far[np.random.randint(len(far))]
    return np.exp2(a.ravel()).repeat(32)


def f64(x):
    return np.asarray(x).astype(np.float64)


def striped(idx):
    return np.tile(idx.reshape(-1, 16).T, (8, 1)).astype(np.uint16)


def unstriped(offs):
    return offs[:16].T.reshape(-1).astype(np.int64)


def silu(v):
    return v / (1.0 + np.exp(-np.maximum(v, -700.0)))


K, T, E, C, H, N = 512, 512, 8, 256, 512, 128
TOP = 4


def by_expert(wq, xq):
    return np.concatenate([wq[e].T @ xq[:, e * C:(e + 1) * C] for e in range(E)], axis=1)


def setup_inputs():
    n = np.random.standard_normal
    s = mx_kscale(K)[:, None]
    u = mx_kscale(H)
    deal = np.repeat(np.arange(E), C).reshape(TOP, T)[:, np.random.permutation(T)]
    deal = np.take_along_axis(deal, np.argsort(np.random.rand(TOP, T), axis=0), axis=0)
    for _ in range(8):
        s_, t_ = np.random.permutation(T).reshape(2, -1); r = np.random.randint(TOP, size=T // 2); x, y = deal[r, s_].copy(), deal[r, t_].copy()
        ok = ~((deal[:, s_] == y).any(0) | (deal[:, t_] == x).any(0)); deal[r[ok], s_[ok]] = y[ok]; deal[r[ok], t_[ok]] = x[ok]
    order = np.lexsort((np.random.rand(TOP * T), deal.reshape(-1)))
    slot_token = order % T; pos = np.empty(TOP * T, np.int64); pos[order] = np.arange(TOP * T); pos = pos.reshape(TOP, T)
    g = np.random.uniform(0.5, 1.5, (TOP, T)); g = g / g.sum(0)
    w_slot = np.empty(E * C)
    for r in range(TOP): w_slot[pos[r]] = g[r]
    return {
        "xT": (n((K, T)) * s).astype(np.float32),
        "w1": (n((E, K, H)) / np.sqrt(K) / s[None]).astype(np.float32),
        "w3": (n((E, K, H)) / np.sqrt(K) / s[None] * u[None, None, :]).astype(np.float32),
        "w2": (n((E, H, N)) / np.sqrt(H) / u[None, :, None]).astype(np.float32),
        "gate": np.tile(w_slot, (K, 1)).astype(np.float32),
        "offs": striped(slot_token),
        "pos1": striped(pos[0]),
        "pos2": striped(pos[1]),
        "pos3": striped(pos[2]),
        "pos4": striped(pos[3]),
    }


def reference(xT, w1, w3, w2, gate, offs, pos1, pos2, pos3, pos4):
    idx = unstriped(offs)
    xq = mxq(f64(gate) * f64(xT)[:, idx], 0, "e4m3")
    h = silu(by_expert(mxq(f64(w1), 1, "e4m3"), xq))
    h = h * by_expert(mxq(f64(w3), 1, "e4m3"), xq)
    y = by_expert(mxq(f64(w2), 1, "e4m3"), mxq(h, 0, "e4m3"))
    return y[:, unstriped(pos1)] + y[:, unstriped(pos2)] + y[:, unstriped(pos3)] + y[:, unstriped(pos4)]

@@ -1,0 +1,228 @@
+from contextlib import ExitStack
+
+import concourse.mybir as mybir
+
+K, T, E, C, H, N = 512, 512, 8, 256, 512, 128
+S = E * C
+FLOPS = 2 * S * (2 * K * H + H * N)
+BYTES = 4 * (K * T + 2 * E * K * H + E * H * N + S + N * T) + 2 * (S + 4 * T)
+
+F32 = mybir.dt.float32
+BF16 = mybir.dt.bfloat16
+U32 = mybir.dt.uint32
+U16 = mybir.dt.uint16
+U8 = mybir.dt.uint8
+FP8X4 = mybir.dt.float8_e4m3fn_x4
+MULT = mybir.AluOpType.mult
+ADD = mybir.AluOpType.add
+SILU = mybir.ActivationFunctionType.Silu
+
+P = 128
+PACK = 4
+HALF = 128
+
+
+def tile_moe_pre_glu_silu_kernel(tc, xT, w1, w3, w2, gate, offs, pos1, pos2, pos3, pos4, out):
+    nc = tc.nc
+    with ExitStack() as ctx:
+        keep = ctx.enter_context(tc.tile_pool(name="keep", bufs=1))
+        raw = ctx.enter_context(tc.tile_pool(name="raw", bufs=4))
+        one = ctx.enter_context(tc.tile_pool(name="one", bufs=1))
+        two = ctx.enter_context(tc.tile_pool(name="two", bufs=2))
+        psum3 = ctx.enter_context(tc.psum_pool(name="psum3", bufs=3))
+        psum2 = ctx.enter_context(tc.psum_pool(name="psum2", bufs=2))
+
+        offs_sb = keep.tile([P, S // 16], U16, name="offs_sb")
+        pos_sb = [keep.tile([P, T // 16], U16, name="pos%d_sb" % r) for r in range(4)]
+        planes = [keep.tile([P, T], F32, name="plane%d" % t) for t in range(PACK)]
+        gates = [keep.tile([P, 2 * C], F32, name="gate%d" % g) for g in range(E // 2)]
+        y_sb = keep.tile([P, S], F32, name="y_sb")
+        x_rows = xT.rearrange("(p j) c -> p j c", j=PACK)
+
+        warm_in = keep.tile([P, 1], F32, name="warm_in")
+        warm_out = keep.tile([P, 1], F32, name="warm_out")
+        nc.gpsimd.memset(warm_in[:], 0.0)
+        nc.scalar.activation(warm_out[:], warm_in[:], SILU)
+
+        raws = {}
+
+        def load_first(w, e, tag, half):
+            t = raw.tile([P, PACK, H // 2], F32, name=tag + "ab"[half])
+            nc.sync.dma_start(t[:], w[e].rearrange("(p j) c -> p j c", j=PACK)[:, :, half * (H // 2):(half + 1) * (H // 2)])
+            raws[(tag, e, half)] = t
+
+        def load_w2(e):
+            t = raw.tile([P, PACK, N], F32, name="w2raw")
+            nc.sync.dma_start(t[:], w2[e].rearrange("(p j) c -> p j c", j=PACK))
+            raws[("w2", e)] = t
+
+        def load_gate(g):
+            nc.sync.dma_start(gates[g][:], gate[0:P, g * 2 * C:(g + 1) * 2 * C])
+
+        def load_expert(e):
+            load_first(w1, e, "w1", 0)
+            load_first(w1, e, "w1", 1)
+            load_first(w3, e, "w3", 0)
+            load_first(w3, e, "w3", 1)
+            load_w2(e)
+
+        nc.sync.dma_start(offs_sb[:], offs)
+        for t in range(PACK):
+            load_first(w1 if t < 2 else w3, 0, "w1" if t < 2 else "w3", t % 2)
+            nc.sync.dma_start(planes[t][:], x_rows[:, t, :])
+        load_gate(0)
+        load_w2(0)
+
+        state = {}
+
+        def gather_x(e):
+            g = two.tile([P, PACK, C], F32, name="gathered")
+            for t in range(PACK):
+                nc.vector.tensor_copy(g[:, t, :], planes[t][:].indirect(offs_sb[:, e * (C // 16):(e + 1) * (C // 16)]))
+            state[("g", e)] = g
+
+        def gate_x(e):
+            g = state[("g", e)]
+            xb = one.tile([P, C, PACK], BF16, name="x_bf", align_bytes=64)
+            gt = gates[e // 2][:, (e % 2) * C:(e % 2 + 1) * C]
+            nc.vector.tensor_tensor(
+                xb[:].rearrange("p (a i) t -> p a t i", i=4),
+                g[:].rearrange("p t (a i) -> p a t i", i=4),
+                gt.rearrange("p (a i) -> p a i", i=4).unsqueeze(2).to_broadcast([P, C // 4, PACK, 4]),
+                MULT,
+            )
+            state[("xb", e)] = xb
+
+        def quantize(src, width, tag, pool):
+            codes = pool.tile([P, width], U32, name=tag + "_codes", align_bytes=64)
+            scales = pool.tile([P, width], U8, name=tag + "_scales", align_bytes=64)
+            nc.vector.quantize_mx(out=codes[:].bitcast(FP8X4), scales=scales[:], in_=src)
+            return codes, scales
+
+        def quant_x(e):
+            state[("xq", e)] = quantize(state[("xb", e)][:].rearrange("p s t -> p (s t)"), C, "x", two)
+
+        def cast_first(e, tag):
+            wb = two.tile([P, PACK, P, PACK], BF16, name=tag + "_bf", align_bytes=64)
+            for half in range(2):
+                nc.scalar.copy(
+                    wb[:, :, half * 64:(half + 1) * 64, :].rearrange("p t m j -> p m j t"),
+                    raws[(tag, e, half)][:].rearrange("p j (m t) -> p m j t", t=PACK),
+                )
+            state[(tag + "b", e)] = wb
+
+        def quant_first(e, tag):
+            state[(tag + "q", e)] = quantize(state[(tag + "b", e)][:].rearrange("p t m j -> p (t m j)"), H, tag, two)
+
+        def cast_w2(e):
+            wb = two.tile([P, N, PACK], BF16, name="w2_bf", align_bytes=64)
+            nc.vector.tensor_copy(
+                wb[:].rearrange("p (a i) j -> p a j i", i=4),
+                raws[("w2", e)][:].rearrange("p j (a i) -> p a j i", i=4),
+            )
+            state[("w2b", e)] = wb
+
+        def quant_w2(e):
+            state[("w2q", e)] = quantize(state[("w2b", e)][:].rearrange("p n j -> p (n j)"), N, "w2", two)
+
+        def product(e, tag, half):
+            acc = psum3.tile([P, PACK, HALF], F32, name=tag + "_acc")
+            wc, ws = state[(tag + "q", e)]
+            xc, xs = state[("xq", e)]
+            cols = slice(half * HALF, (half + 1) * HALF)
+            for t in range(PACK):
+                nc.tensor.matmul_mx(
+                    out=acc[:, t, :],
+                    lhsT=wc[:, t * P:(t + 1) * P].bitcast(FP8X4),
+                    lhsT_scale=ws[:, t * P:(t + 1) * P],
+                    rhs=xc[:, cols].bitcast(FP8X4),
+                    rhs_scale=xs[:, cols],
+                    start=True,
+                    stop=True,
+                )
+            state[(tag + "acc", e, half)] = acc
+
+        def silu(e, half):
+            sil = two.tile([P, HALF, PACK], F32, name="silu")
+            nc.scalar.activation(sil[:], state[("w1acc", e, half)][:].rearrange("p t s -> p s t"), SILU)
+            state[("sil", e, half)] = sil
+
+        def hidden(e, half):
+            if half == 0:
+                state[("hb", e)] = two.tile([P, C, PACK], BF16, name="h_bf", align_bytes=64)
+            nc.vector.tensor_tensor(
+                state[("hb", e)][:, half * HALF:(half + 1) * HALF, :],
+                state[("w3acc", e, half)][:].rearrange("p t s -> p s t"),
+                state[("sil", e, half)][:],
+                MULT,
+            )
+
+        def second(e):
+            hc, hs = quantize(state[("hb", e)][:].rearrange("p s t -> p (s t)"), C, "h", two)
+            wc, ws = state[("w2q", e)]
+            acc = psum2.tile([P, C], F32, name="y_acc")
+            nc.tensor.matmul_mx(
+                out=acc[:], lhsT=wc[:].bitcast(FP8X4), lhsT_scale=ws[:],
+                rhs=hc[:].bitcast(FP8X4), rhs_scale=hs[:], start=True, stop=True,
+            )
+            state[("yacc", e)] = acc
+
+        def copy_y(e):
+            nc.scalar.copy(y_sb[:, e * C:(e + 1) * C], state[("yacc", e)][:])
+
+        load_expert(1)
+        cast_first(0, "w1")
+        gather_x(0)
+        quant_first(0, "w1")
+        gate_x(0)
+        cast_first(0, "w3")
+        cast_w2(0)
+        quant_x(0)
+        quant_w2(0)
+        for e in range(E):
+            nxt = e + 1 < E
+            if e + 2 < E:
+                if e % 2 == 0:
+                    load_gate(e // 2 + 1)
+                load_expert(e + 2)
+            if e == 4:
+                for r, pos in enumerate((pos1, pos2, pos3, pos4)):
+                    nc.sync.dma_start(pos_sb[r][:], pos)
+            quant_first(e, "w3")
+            for half in range(2):
+                product(e, "w1", half)
+                product(e, "w3", half)
+            if nxt:
+                cast_first(e + 1, "w1")
+                gather_x(e + 1)
+            if e > 0:
+                copy_y(e - 1)
+            silu(e, 0)
+            silu(e, 1)
+            if nxt:
+                quant_first(e + 1, "w1")
+            hidden(e, 0)
+            if nxt:
+                gate_x(e + 1)
+                cast_first(e + 1, "w3")
+            hidden(e, 1)
+            if nxt:
+                cast_w2(e + 1)
+                quant_x(e + 1)
+            second(e)
+            if nxt:
+                quant_w2(e + 1)
+        copy_y(E - 1)
+
+        sums = {}
+        for r in range(4):
+            for half in range(2):
+                picks = y_sb[:].indirect(pos_sb[r][:, half * 16:(half + 1) * 16])
+                s = keep.tile([P, T // 2], F32, name="sum%d%d" % (r, half))
+                if r == 0:
+                    nc.vector.tensor_copy(s[:], picks)
+                else:
+                    nc.vector.tensor_tensor(s[:], picks, sums[half][:], ADD)
+                sums[half] = s
+                if r == 3:
+                    nc.sync.dma_start(out[:, half * (T // 2):(half + 1) * (T // 2)], s[:])

@@ -20,6 +20,10 @@ SILU = mybir.ActivationFunctionType.Silu
 P = 128
 PACK = 4
 HALF = 128
+LEAD = 3
+C2 = 2 * C
+ON_VECTOR = ((7, 1),)
+W2_ON_VECTOR = (3,)
 
 
 def tile_moe_pre_glu_silu_kernel(tc, xT, w1, w3, w2, gate, offs, pos1, pos2, pos3, pos4, out):
@@ -29,66 +33,87 @@ def tile_moe_pre_glu_silu_kernel(tc, xT, w1, w3, w2, gate, offs, pos1, pos2, pos
         raw = ctx.enter_context(tc.tile_pool(name="raw", bufs=4))
         one = ctx.enter_context(tc.tile_pool(name="one", bufs=1))
         two = ctx.enter_context(tc.tile_pool(name="two", bufs=2))
+        three = ctx.enter_context(tc.tile_pool(name="three", bufs=3))
+        four = ctx.enter_context(tc.tile_pool(name="four", bufs=4))
         psum3 = ctx.enter_context(tc.psum_pool(name="psum3", bufs=3))
         psum2 = ctx.enter_context(tc.psum_pool(name="psum2", bufs=2))
 
         offs_sb = keep.tile([P, S // 16], U16, name="offs_sb")
         pos_sb = [keep.tile([P, T // 16], U16, name="pos%d_sb" % r) for r in range(4)]
         planes = [keep.tile([P, T], F32, name="plane%d" % t) for t in range(PACK)]
-        gates = [keep.tile([P, 2 * C], F32, name="gate%d" % g) for g in range(E // 2)]
+        gates = [keep.tile([P, C2], F32, name="gate%d" % g) for g in range(E // 2)]
         y_sb = keep.tile([P, S], F32, name="y_sb")
         x_rows = xT.rearrange("(p j) c -> p j c", j=PACK)
 
-        warm_in = keep.tile([P, 1], F32, name="warm_in")
         warm_out = keep.tile([P, 1], F32, name="warm_out")
+        warm_in = keep.tile([P, 1], F32, name="warm_in")
         nc.gpsimd.memset(warm_in[:], 0.0)
         nc.scalar.activation(warm_out[:], warm_in[:], SILU)
 
         raws = {}
 
-        def load_first(w, e, tag, half):
-            t = raw.tile([P, PACK, H // 2], F32, name=tag + "ab"[half])
-            nc.sync.dma_start(t[:], w[e].rearrange("(p j) c -> p j c", j=PACK)[:, :, half * (H // 2):(half + 1) * (H // 2)])
-            raws[(tag, e, half)] = t
+        def load_first(w, e, tag, parts):
+            width = H // parts
+            rows = w[e].rearrange("(p j) c -> p j c", j=PACK)
+            pool = raw if parts == 1 else keep
+            for part in range(parts):
+                t = pool.tile([P, PACK, width], F32, name=tag + ("" if parts == 1 else "ab"[part]))
+                raws[(tag, e, part)] = (t, rows[:, :, part * width:(part + 1) * width])
+            raws[(tag, e)] = parts
 
-        def load_w2(e):
-            t = raw.tile([P, PACK, N], F32, name="w2raw")
-            nc.sync.dma_start(t[:], w2[e].rearrange("(p j) c -> p j c", j=PACK))
-            raws[("w2", e)] = t
+        def start(key):
+            t, src = raws[key]
+            nc.sync.dma_start(t[:], src)
+
+        def load_w2(g):
+            t = two.tile([P, 2, PACK * N], F32, name="w2raw")
+            nc.sync.dma_start(t[:], w2[2 * g:2 * g + 2].rearrange("e (p j) c -> p e (j c)", j=PACK))
+            raws[("w2", g)] = t
 
         def load_gate(g):
-            nc.sync.dma_start(gates[g][:], gate[0:P, g * 2 * C:(g + 1) * 2 * C])
+            nc.sync.dma_start(gates[g][:], gate[0:P, g * C2:(g + 1) * C2])
+
+        def load_plane(t):
+            nc.sync.dma_start(planes[t][:], x_rows[:, t, :])
 
         def load_expert(e):
-            load_first(w1, e, "w1", 0)
             load_first(w1, e, "w1", 1)
-            load_first(w3, e, "w3", 0)
+            start(("w1", e, 0))
             load_first(w3, e, "w3", 1)
-            load_w2(e)
+            start(("w3", e, 0))
 
+        load_first(w1, 0, "w1", 2)
+        load_first(w3, 0, "w3", 2)
         nc.sync.dma_start(offs_sb[:], offs)
-        for t in range(PACK):
-            load_first(w1 if t < 2 else w3, 0, "w1" if t < 2 else "w3", t % 2)
-            nc.sync.dma_start(planes[t][:], x_rows[:, t, :])
+        load_plane(0)
+        start(("w1", 0, 0))
+        load_plane(1)
+        start(("w1", 0, 1))
+        load_plane(2)
+        load_plane(3)
         load_gate(0)
-        load_w2(0)
+        start(("w3", 0, 0))
+        start(("w3", 0, 1))
 
         state = {}
 
         def gather_x(e):
-            g = two.tile([P, PACK, C], F32, name="gathered")
+            if e < LEAD:
+                gt = keep.tile([P, PACK, C], F32, name="gathered%d" % e)[:]
+            else:
+                spent = raws[("w3", e - LEAD + 1, 0)][0]
+                gt = spent[:].rearrange("p j c -> p (j c)")[:, :PACK * C].rearrange("p (t s) -> p t s", t=PACK)
             for t in range(PACK):
-                nc.vector.tensor_copy(g[:, t, :], planes[t][:].indirect(offs_sb[:, e * (C // 16):(e + 1) * (C // 16)]))
-            state[("g", e)] = g
+                nc.vector.tensor_copy(gt[:, t, :], planes[t][:].indirect(offs_sb[:, e * (C // 16):(e + 1) * (C // 16)]))
+            state[("g", e)] = gt
 
         def gate_x(e):
-            g = state[("g", e)]
-            xb = one.tile([P, C, PACK], BF16, name="x_bf", align_bytes=64)
-            gt = gates[e // 2][:, (e % 2) * C:(e % 2 + 1) * C]
+            cols = slice((e % 2) * C, (e % 2 + 1) * C)
+            xb = two.tile([P, C, PACK], BF16, name="x_bf", align_bytes=64)
             nc.vector.tensor_tensor(
                 xb[:].rearrange("p (a i) t -> p a t i", i=4),
-                g[:].rearrange("p t (a i) -> p a t i", i=4),
-                gt.rearrange("p (a i) -> p a i", i=4).unsqueeze(2).to_broadcast([P, C // 4, PACK, 4]),
+                state[("g", e)].rearrange("p t (a i) -> p a t i", i=4),
+                gates[e // 2][:, cols].rearrange("p (a i) -> p a i", i=4).unsqueeze(2).to_broadcast([P, C // 4, PACK, 4]),
                 MULT,
             )
             state[("xb", e)] = xb
@@ -100,51 +125,57 @@ def tile_moe_pre_glu_silu_kernel(tc, xT, w1, w3, w2, gate, offs, pos1, pos2, pos
             return codes, scales
 
         def quant_x(e):
-            state[("xq", e)] = quantize(state[("xb", e)][:].rearrange("p s t -> p (s t)"), C, "x", two)
+            state[("xq", e)] = quantize(state[("xb", e)][:].rearrange("p s t -> p (s t)"), C, "x", four)
 
-        def cast_first(e, tag):
-            wb = two.tile([P, PACK, P, PACK], BF16, name=tag + "_bf", align_bytes=64)
-            for half in range(2):
-                nc.scalar.copy(
-                    wb[:, :, half * 64:(half + 1) * 64, :].rearrange("p t m j -> p m j t"),
-                    raws[(tag, e, half)][:].rearrange("p j (m t) -> p m j t", t=PACK),
+        def cast_first(e, which):
+            tag = ("w1", "w3")[which]
+            if which == 0:
+                state[("wb", e)] = three.tile([P, 2, PACK, P, PACK], BF16, name="w_bf", align_bytes=64)
+            parts = raws[(tag, e)]
+            for part in range(parts):
+                ms = slice(part * (P // parts), (part + 1) * (P // parts))
+                copy = nc.vector.tensor_copy if (e, which) in ON_VECTOR else nc.scalar.copy
+                copy(
+                    state[("wb", e)][:, which, :, ms, :].rearrange("p t m j -> p m j t"),
+                    raws[(tag, e, part)][0][:].rearrange("p j (m t) -> p m j t", t=PACK),
                 )
-            state[(tag + "b", e)] = wb
 
-        def quant_first(e, tag):
-            state[(tag + "q", e)] = quantize(state[(tag + "b", e)][:].rearrange("p t m j -> p (t m j)"), H, tag, two)
+        def quant_first(e):
+            state[("wq", e)] = quantize(state[("wb", e)][:].rearrange("p w t m j -> p (w t m j)"), 2 * H, "w", two)
 
-        def cast_w2(e):
-            wb = two.tile([P, N, PACK], BF16, name="w2_bf", align_bytes=64)
-            nc.vector.tensor_copy(
-                wb[:].rearrange("p (a i) j -> p a j i", i=4),
-                raws[("w2", e)][:].rearrange("p j (a i) -> p a j i", i=4),
+        def cast_w2(g):
+            wb = one.tile([P, 2, N, PACK], BF16, name="w2_bf", align_bytes=64)
+            copy = nc.vector.tensor_copy if g in W2_ON_VECTOR else nc.scalar.copy
+            copy(
+                wb[:].rearrange("p e (a i) j -> p e a j i", i=4),
+                raws[("w2", g)][:].rearrange("p e (j a i) -> p e a j i", i=4, j=PACK),
             )
-            state[("w2b", e)] = wb
+            state[("w2b", g)] = wb
 
-        def quant_w2(e):
-            state[("w2q", e)] = quantize(state[("w2b", e)][:].rearrange("p n j -> p (n j)"), N, "w2", two)
+        def quant_w2(g):
+            state[("w2q", g)] = quantize(state[("w2b", g)][:].rearrange("p e n j -> p (e n j)"), 2 * N, "w2", two)
 
-        def product(e, tag, half):
-            acc = psum3.tile([P, PACK, HALF], F32, name=tag + "_acc")
-            wc, ws = state[(tag + "q", e)]
+        def product(e, which, half):
+            acc = psum3.tile([P, PACK, HALF], F32, name="acc%d" % which)
+            wc, ws = state[("wq", e)]
             xc, xs = state[("xq", e)]
             cols = slice(half * HALF, (half + 1) * HALF)
             for t in range(PACK):
+                ch = slice(which * H + t * P, which * H + (t + 1) * P)
                 nc.tensor.matmul_mx(
                     out=acc[:, t, :],
-                    lhsT=wc[:, t * P:(t + 1) * P].bitcast(FP8X4),
-                    lhsT_scale=ws[:, t * P:(t + 1) * P],
+                    lhsT=wc[:, ch].bitcast(FP8X4),
+                    lhsT_scale=ws[:, ch],
                     rhs=xc[:, cols].bitcast(FP8X4),
                     rhs_scale=xs[:, cols],
                     start=True,
                     stop=True,
                 )
-            state[(tag + "acc", e, half)] = acc
+            state[("acc", which, e, half)] = acc
 
         def silu(e, half):
-            sil = two.tile([P, HALF, PACK], F32, name="silu")
-            nc.scalar.activation(sil[:], state[("w1acc", e, half)][:].rearrange("p t s -> p s t"), SILU)
+            sil = four.tile([P, HALF, PACK], F32, name="silu")
+            nc.scalar.activation(sil[:], state[("acc", 0, e, half)][:].rearrange("p t s -> p s t"), SILU)
             state[("sil", e, half)] = sil
 
         def hidden(e, half):
@@ -152,17 +183,18 @@ def tile_moe_pre_glu_silu_kernel(tc, xT, w1, w3, w2, gate, offs, pos1, pos2, pos
                 state[("hb", e)] = two.tile([P, C, PACK], BF16, name="h_bf", align_bytes=64)
             nc.vector.tensor_tensor(
                 state[("hb", e)][:, half * HALF:(half + 1) * HALF, :],
-                state[("w3acc", e, half)][:].rearrange("p t s -> p s t"),
+                state[("acc", 1, e, half)][:].rearrange("p t s -> p s t"),
                 state[("sil", e, half)][:],
                 MULT,
             )
 
         def second(e):
             hc, hs = quantize(state[("hb", e)][:].rearrange("p s t -> p (s t)"), C, "h", two)
-            wc, ws = state[("w2q", e)]
+            wc, ws = state[("w2q", e // 2)]
+            ch = slice((e % 2) * N, (e % 2 + 1) * N)
             acc = psum2.tile([P, C], F32, name="y_acc")
             nc.tensor.matmul_mx(
-                out=acc[:], lhsT=wc[:].bitcast(FP8X4), lhsT_scale=ws[:],
+                out=acc[:], lhsT=wc[:, ch].bitcast(FP8X4), lhsT_scale=ws[:, ch],
                 rhs=hc[:].bitcast(FP8X4), rhs_scale=hs[:], start=True, stop=True,
             )
             state[("yacc", e)] = acc
@@ -171,47 +203,54 @@ def tile_moe_pre_glu_silu_kernel(tc, xT, w1, w3, w2, gate, offs, pos1, pos2, pos
             nc.scalar.copy(y_sb[:, e * C:(e + 1) * C], state[("yacc", e)][:])
 
         load_expert(1)
-        cast_first(0, "w1")
-        gather_x(0)
-        quant_first(0, "w1")
-        gate_x(0)
-        cast_first(0, "w3")
-        cast_w2(0)
-        quant_x(0)
-        quant_w2(0)
-        for e in range(E):
+        load_gate(1)
+        load_w2(0)
+        for e in range(LEAD - 1):
+            gather_x(e)
+        for e in range(LEAD - 1):
+            gate_x(e)
+            quant_x(e)
+        for e in range(-1, E):
             nxt = e + 1 < E
-            if e + 2 < E:
-                if e % 2 == 0:
-                    load_gate(e // 2 + 1)
-                load_expert(e + 2)
-            if e == 4:
+            ahead = e + LEAD < E
+            if e + 3 < E:
+                load_expert(e + 3)
+            if e in (-1, 1):
+                load_gate((e + 5) // 2)
+            if e % 2 == 0 and e + 2 < E:
+                load_w2(e // 2 + 1)
+            if e == 3:
                 for r, pos in enumerate((pos1, pos2, pos3, pos4)):
                     nc.sync.dma_start(pos_sb[r][:], pos)
-            quant_first(e, "w3")
-            for half in range(2):
-                product(e, "w1", half)
-                product(e, "w3", half)
             if nxt:
-                cast_first(e + 1, "w1")
-                gather_x(e + 1)
+                cast_first(e + 1, 0)
+                cast_first(e + 1, 1)
+            if e >= 0:
+                silu(e, 0)
+                silu(e, 1)
             if e > 0:
                 copy_y(e - 1)
-            silu(e, 0)
-            silu(e, 1)
+            if e % 2 == 1 and nxt:
+                cast_w2((e + 1) // 2)
             if nxt:
-                quant_first(e + 1, "w1")
-            hidden(e, 0)
-            if nxt:
-                gate_x(e + 1)
-                cast_first(e + 1, "w3")
-            hidden(e, 1)
-            if nxt:
-                cast_w2(e + 1)
-                quant_x(e + 1)
-            second(e)
-            if nxt:
-                quant_w2(e + 1)
+                quant_first(e + 1)
+                for half in range(2):
+                    product(e + 1, 0, half)
+                    product(e + 1, 1, half)
+            if e >= 0:
+                hidden(e, 0)
+            if ahead:
+                gather_x(e + LEAD)
+            if e >= 0:
+                hidden(e, 1)
+            if ahead:
+                gate_x(e + LEAD)
+            if e >= 0:
+                second(e)
+            if ahead:
+                quant_x(e + LEAD)
+            if e % 2 == 1 and nxt:
+                quant_w2((e + 1) // 2)
         copy_y(E - 1)
 
         sums = {}

@@ -1,6 +1,7 @@
 from contextlib import ExitStack
 
 import concourse.mybir as mybir
+from concourse.masks import make_identity
 
 K, T, E, C, H, N = 512, 512, 8, 256, 512, 128
 S = E * C
@@ -15,15 +16,18 @@ U8 = mybir.dt.uint8
 FP8X4 = mybir.dt.float8_e4m3fn_x4
 MULT = mybir.AluOpType.mult
 ADD = mybir.AluOpType.add
+COPY = mybir.ActivationFunctionType.Copy
 SILU = mybir.ActivationFunctionType.Silu
 
 P = 128
 PACK = 4
 HALF = 128
+DIRECT = 3
 LEAD = 3
 C2 = 2 * C
-ON_VECTOR = ((7, 1),)
-W2_ON_VECTOR = (3,)
+VECTOR_SHARE = {(6, 0): 128, (7, 0): 128}
+WORDS_ON_VECTOR = ()
+W2_ON_VECTOR = (0, 1, 2, 3)
 
 
 def tile_moe_pre_glu_silu_kernel(tc, xT, w1, w3, w2, gate, offs, pos1, pos2, pos3, pos4, out):
@@ -35,13 +39,17 @@ def tile_moe_pre_glu_silu_kernel(tc, xT, w1, w3, w2, gate, offs, pos1, pos2, pos
         two = ctx.enter_context(tc.tile_pool(name="two", bufs=2))
         three = ctx.enter_context(tc.tile_pool(name="three", bufs=3))
         four = ctx.enter_context(tc.tile_pool(name="four", bufs=4))
-        psum3 = ctx.enter_context(tc.psum_pool(name="psum3", bufs=3))
         psum2 = ctx.enter_context(tc.psum_pool(name="psum2", bufs=2))
+        psum1 = ctx.enter_context(tc.psum_pool(name="psum1", bufs=1))
 
         offs_sb = keep.tile([P, S // 16], U16, name="offs_sb")
         pos_sb = [keep.tile([P, T // 16], U16, name="pos%d_sb" % r) for r in range(4)]
         planes = [keep.tile([P, T], F32, name="plane%d" % t) for t in range(PACK)]
-        gates = [keep.tile([P, C2], F32, name="gate%d" % g) for g in range(E // 2)]
+        gate_rows = keep.tile([P, P], F32, name="gate_rows")
+        gate_cols = keep.tile([P, S // P], F32, name="gate_cols")
+        gate_wide = keep.tile([P, DIRECT * C], F32, name="gate_wide")
+        ident = keep.tile([P, P], F32, name="ident")
+        make_identity(nc, ident[:])
         y_sb = keep.tile([P, S], F32, name="y_sb")
         x_rows = xT.rearrange("(p j) c -> p j c", j=PACK)
 
@@ -70,8 +78,14 @@ def tile_moe_pre_glu_silu_kernel(tc, xT, w1, w3, w2, gate, offs, pos1, pos2, pos
             nc.sync.dma_start(t[:], w2[2 * g:2 * g + 2].rearrange("e (p j) c -> p e (j c)", j=PACK))
             raws[("w2", g)] = t
 
-        def load_gate(g):
-            nc.sync.dma_start(gates[g][:], gate[0:P, g * C2:(g + 1) * C2])
+        def load_gate():
+            nc.sync.dma_start(gate_rows[:], gate[0:P * P // S, :].rearrange("r (c s) -> (r c) s", s=P))
+            turned = psum2.tile([P, PACK, P], F32, name="x_turned")
+            nc.tensor.transpose(turned[:, 0, :], gate_rows[:], ident[:])
+            nc.scalar.copy(gate_cols[:], turned[:, 0, :S // P])
+
+        def load_gate_wide(lo, hi):
+            nc.sync.dma_start(gate_wide[:, lo * C:hi * C], gate[0:P, lo * C:hi * C])
 
         def load_plane(t):
             nc.sync.dma_start(planes[t][:], x_rows[:, t, :])
@@ -91,8 +105,9 @@ def tile_moe_pre_glu_silu_kernel(tc, xT, w1, w3, w2, gate, offs, pos1, pos2, pos
         start(("w1", 0, 1))
         load_plane(2)
         load_plane(3)
-        load_gate(0)
+        load_gate_wide(0, 2)
         start(("w3", 0, 0))
+        load_gate()
         start(("w3", 0, 1))
 
         state = {}
@@ -108,13 +123,37 @@ def tile_moe_pre_glu_silu_kernel(tc, xT, w1, w3, w2, gate, offs, pos1, pos2, pos
             state[("g", e)] = gt
 
         def gate_x(e):
-            cols = slice((e % 2) * C, (e % 2 + 1) * C)
-            xb = two.tile([P, C, PACK], BF16, name="x_bf", align_bytes=64)
+            back = psum1.tile([P, 2, 2, HALF], F32, name="x_back")
+            for half in range(2):
+                turned = psum2.tile([P, PACK, P], F32, name="x_turned")
+                for t in range(PACK):
+                    nc.tensor.transpose(turned[:, t, :], state[("g", e)][:, t, half * HALF:(half + 1) * HALF], ident[:])
+                rows = two.tile([P, 2, P, 2], BF16, name="x_rows_bf")
+                chunk = 2 * e + half
+                nc.scalar.activation(
+                    rows[:], turned[:].rearrange("s (u v) p -> s u p v", v=2), COPY, scale=gate_cols[:, chunk:chunk + 1]
+                )
+                words = rows[:].rearrange("s u p v -> s (u p v)").bitcast(F32)
+                for u in range(2):
+                    nc.tensor.transpose(back[:, half, u, :], words[:, u * P:(u + 1) * P], ident[:])
+            state[("back", e)] = back
+
+        def gate_x_direct(e):
+            xb = two.tile([P, C * PACK], BF16, name="x_bf", align_bytes=64)
             nc.vector.tensor_tensor(
-                xb[:].rearrange("p (a i) t -> p a t i", i=4),
+                xb[:].rearrange("p (a i t) -> p a t i", i=4, t=PACK),
                 state[("g", e)].rearrange("p t (a i) -> p a t i", i=4),
-                gates[e // 2][:, cols].rearrange("p (a i) -> p a i", i=4).unsqueeze(2).to_broadcast([P, C // 4, PACK, 4]),
+                gate_wide[:, e * C:(e + 1) * C].rearrange("p (a i) -> p a i", i=4).unsqueeze(2).to_broadcast([P, C // 4, PACK, 4]),
                 MULT,
+            )
+            state[("xb", e)] = xb
+
+        def words_x(e):
+            xb = two.tile([P, C * PACK], BF16, name="x_bf", align_bytes=64)
+            copy = nc.vector.tensor_copy if e in WORDS_ON_VECTOR else nc.scalar.copy
+            copy(
+                xb[:].bitcast(F32).rearrange("p (h s u) -> p h s u", h=2, u=2),
+                state[("back", e)][:].rearrange("p h u s -> p h s u"),
             )
             state[("xb", e)] = xb
 
@@ -125,20 +164,22 @@ def tile_moe_pre_glu_silu_kernel(tc, xT, w1, w3, w2, gate, offs, pos1, pos2, pos
             return codes, scales
 
         def quant_x(e):
-            state[("xq", e)] = quantize(state[("xb", e)][:].rearrange("p s t -> p (s t)"), C, "x", four)
+            state[("xq", e)] = quantize(state[("xb", e)][:], C, "x", four)
 
         def cast_first(e, which):
             tag = ("w1", "w3")[which]
             if which == 0:
                 state[("wb", e)] = three.tile([P, 2, PACK, P, PACK], BF16, name="w_bf", align_bytes=64)
             parts = raws[(tag, e)]
+            width = P // parts
             for part in range(parts):
-                ms = slice(part * (P // parts), (part + 1) * (P // parts))
-                copy = nc.vector.tensor_copy if (e, which) in ON_VECTOR else nc.scalar.copy
-                copy(
-                    state[("wb", e)][:, which, :, ms, :].rearrange("p t m j -> p m j t"),
-                    raws[(tag, e, part)][0][:].rearrange("p j (m t) -> p m j t", t=PACK),
-                )
+                cut = VECTOR_SHARE.get((e, which), 0) if parts == 1 else 0
+                for copy, lo, hi in ((nc.vector.tensor_copy, 0, cut), (nc.scalar.copy, cut, width)):
+                    if hi > lo:
+                        copy(
+                            state[("wb", e)][:, which, :, part * width + lo:part * width + hi, :].rearrange("p t m j -> p m j t"),
+                            raws[(tag, e, part)][0][:].rearrange("p j (m t) -> p m j t", t=PACK)[:, lo:hi],
+                        )
 
         def quant_first(e):
             state[("wq", e)] = quantize(state[("wb", e)][:].rearrange("p w t m j -> p (w t m j)"), 2 * H, "w", two)
@@ -156,7 +197,7 @@ def tile_moe_pre_glu_silu_kernel(tc, xT, w1, w3, w2, gate, offs, pos1, pos2, pos
             state[("w2q", g)] = quantize(state[("w2b", g)][:].rearrange("p e n j -> p (e n j)"), 2 * N, "w2", two)
 
         def product(e, which, half):
-            acc = psum3.tile([P, PACK, HALF], F32, name="acc%d" % which)
+            acc = psum2.tile([P, PACK, HALF], F32, name="acc%d" % which)
             wc, ws = state[("wq", e)]
             xc, xs = state[("xq", e)]
             cols = slice(half * HALF, (half + 1) * HALF)
@@ -192,7 +233,7 @@ def tile_moe_pre_glu_silu_kernel(tc, xT, w1, w3, w2, gate, offs, pos1, pos2, pos
             hc, hs = quantize(state[("hb", e)][:].rearrange("p s t -> p (s t)"), C, "h", two)
             wc, ws = state[("w2q", e // 2)]
             ch = slice((e % 2) * N, (e % 2 + 1) * N)
-            acc = psum2.tile([P, C], F32, name="y_acc")
+            acc = psum1.tile([P, C], F32, name="y_acc")
             nc.tensor.matmul_mx(
                 out=acc[:], lhsT=wc[:, ch].bitcast(FP8X4), lhsT_scale=ws[:, ch],
                 rhs=hc[:].bitcast(FP8X4), rhs_scale=hs[:], start=True, stop=True,
@@ -203,20 +244,19 @@ def tile_moe_pre_glu_silu_kernel(tc, xT, w1, w3, w2, gate, offs, pos1, pos2, pos
             nc.scalar.copy(y_sb[:, e * C:(e + 1) * C], state[("yacc", e)][:])
 
         load_expert(1)
-        load_gate(1)
+        load_gate_wide(2, DIRECT)
         load_w2(0)
         for e in range(LEAD - 1):
             gather_x(e)
-        for e in range(LEAD - 1):
-            gate_x(e)
+        for e in range(LEAD - 2):
+            gate_x_direct(e)
             quant_x(e)
         for e in range(-1, E):
             nxt = e + 1 < E
             ahead = e + LEAD < E
+            turn = e + LEAD - 1
             if e + 3 < E:
                 load_expert(e + 3)
-            if e in (-1, 1):
-                load_gate((e + 5) // 2)
             if e % 2 == 0 and e + 2 < E:
                 load_w2(e // 2 + 1)
             if e == 3:
@@ -228,8 +268,12 @@ def tile_moe_pre_glu_silu_kernel(tc, xT, w1, w3, w2, gate, offs, pos1, pos2, pos
             if e >= 0:
                 silu(e, 0)
                 silu(e, 1)
+            if DIRECT <= turn < E:
+                gate_x(turn)
             if e > 0:
                 copy_y(e - 1)
+            if DIRECT <= turn < E:
+                words_x(turn)
             if e % 2 == 1 and nxt:
                 cast_w2((e + 1) // 2)
             if nxt:
@@ -239,16 +283,15 @@ def tile_moe_pre_glu_silu_kernel(tc, xT, w1, w3, w2, gate, offs, pos1, pos2, pos
                     product(e + 1, 1, half)
             if e >= 0:
                 hidden(e, 0)
-            if ahead:
-                gather_x(e + LEAD)
-            if e >= 0:
                 hidden(e, 1)
             if ahead:
-                gate_x(e + LEAD)
+                gather_x(e + LEAD)
+            if turn < DIRECT:
+                gate_x_direct(turn)
             if e >= 0:
                 second(e)
-            if ahead:
-                quant_x(e + LEAD)
+            if turn < E:
+                quant_x(turn)
             if e % 2 == 1 and nxt:
                 quant_w2((e + 1) // 2)
         copy_y(E - 1)

from contextlib import ExitStack

import concourse.mybir as mybir
from concourse.masks import make_identity

K, T, E, C, H, N = 512, 512, 8, 256, 512, 128
S = E * C
FLOPS = 2 * S * (2 * K * H + H * N)
BYTES = 4 * (K * T + 2 * E * K * H + E * H * N + S + N * T) + 2 * (S + 4 * T)

F32 = mybir.dt.float32
BF16 = mybir.dt.bfloat16
U32 = mybir.dt.uint32
U16 = mybir.dt.uint16
U8 = mybir.dt.uint8
FP8X4 = mybir.dt.float8_e4m3fn_x4
MULT = mybir.AluOpType.mult
ADD = mybir.AluOpType.add
COPY = mybir.ActivationFunctionType.Copy
SILU = mybir.ActivationFunctionType.Silu

P = 128
PACK = 4
HALF = 128
DIRECT = 3
LEAD = 3
C2 = 2 * C
VECTOR_SHARE = {(6, 0): 128, (7, 0): 128}
WORDS_ON_VECTOR = ()
W2_ON_VECTOR = (0, 1, 2, 3)


def tile_moe_pre_glu_silu_kernel(tc, xT, w1, w3, w2, gate, offs, pos1, pos2, pos3, pos4, out):
    nc = tc.nc
    with ExitStack() as ctx:
        keep = ctx.enter_context(tc.tile_pool(name="keep", bufs=1))
        raw = ctx.enter_context(tc.tile_pool(name="raw", bufs=4))
        one = ctx.enter_context(tc.tile_pool(name="one", bufs=1))
        two = ctx.enter_context(tc.tile_pool(name="two", bufs=2))
        three = ctx.enter_context(tc.tile_pool(name="three", bufs=3))
        four = ctx.enter_context(tc.tile_pool(name="four", bufs=4))
        psum2 = ctx.enter_context(tc.psum_pool(name="psum2", bufs=2))
        psum1 = ctx.enter_context(tc.psum_pool(name="psum1", bufs=1))

        offs_sb = keep.tile([P, S // 16], U16, name="offs_sb")
        pos_sb = [keep.tile([P, T // 16], U16, name="pos%d_sb" % r) for r in range(4)]
        planes = [keep.tile([P, T], F32, name="plane%d" % t) for t in range(PACK)]
        gate_rows = keep.tile([P, P], F32, name="gate_rows")
        gate_cols = keep.tile([P, S // P], F32, name="gate_cols")
        gate_wide = keep.tile([P, DIRECT * C], F32, name="gate_wide")
        ident = keep.tile([P, P], F32, name="ident")
        make_identity(nc, ident[:])
        y_sb = keep.tile([P, S], F32, name="y_sb")
        x_rows = xT.rearrange("(p j) c -> p j c", j=PACK)

        warm_out = keep.tile([P, 1], F32, name="warm_out")
        warm_in = keep.tile([P, 1], F32, name="warm_in")
        nc.gpsimd.memset(warm_in[:], 0.0)
        nc.scalar.activation(warm_out[:], warm_in[:], SILU)

        raws = {}

        def load_first(w, e, tag, parts):
            width = H // parts
            rows = w[e].rearrange("(p j) c -> p j c", j=PACK)
            pool = raw if parts == 1 else keep
            for part in range(parts):
                t = pool.tile([P, PACK, width], F32, name=tag + ("" if parts == 1 else "ab"[part]))
                raws[(tag, e, part)] = (t, rows[:, :, part * width:(part + 1) * width])
            raws[(tag, e)] = parts

        def start(key):
            t, src = raws[key]
            nc.sync.dma_start(t[:], src)

        def load_w2(g):
            t = two.tile([P, 2, PACK * N], F32, name="w2raw")
            nc.sync.dma_start(t[:], w2[2 * g:2 * g + 2].rearrange("e (p j) c -> p e (j c)", j=PACK))
            raws[("w2", g)] = t

        def load_gate():
            nc.sync.dma_start(gate_rows[:], gate[0:P * P // S, :].rearrange("r (c s) -> (r c) s", s=P))
            turned = psum2.tile([P, PACK, P], F32, name="x_turned")
            nc.tensor.transpose(turned[:, 0, :], gate_rows[:], ident[:])
            nc.scalar.copy(gate_cols[:], turned[:, 0, :S // P])

        def load_gate_wide(lo, hi):
            nc.sync.dma_start(gate_wide[:, lo * C:hi * C], gate[0:P, lo * C:hi * C])

        def load_plane(t):
            nc.sync.dma_start(planes[t][:], x_rows[:, t, :])

        def load_expert(e):
            load_first(w1, e, "w1", 1)
            start(("w1", e, 0))
            load_first(w3, e, "w3", 1)
            start(("w3", e, 0))

        load_first(w1, 0, "w1", 2)
        load_first(w3, 0, "w3", 2)
        nc.sync.dma_start(offs_sb[:], offs)
        load_plane(0)
        start(("w1", 0, 0))
        load_plane(1)
        start(("w1", 0, 1))
        load_plane(2)
        load_plane(3)
        load_gate_wide(0, 2)
        start(("w3", 0, 0))
        load_gate()
        start(("w3", 0, 1))

        state = {}

        def gather_x(e):
            if e < LEAD:
                gt = keep.tile([P, PACK, C], F32, name="gathered%d" % e)[:]
            else:
                spent = raws[("w3", e - LEAD + 1, 0)][0]
                gt = spent[:].rearrange("p j c -> p (j c)")[:, :PACK * C].rearrange("p (t s) -> p t s", t=PACK)
            for t in range(PACK):
                nc.vector.tensor_copy(gt[:, t, :], planes[t][:].indirect(offs_sb[:, e * (C // 16):(e + 1) * (C // 16)]))
            state[("g", e)] = gt

        def gate_x(e):
            back = psum1.tile([P, 2, 2, HALF], F32, name="x_back")
            for half in range(2):
                turned = psum2.tile([P, PACK, P], F32, name="x_turned")
                for t in range(PACK):
                    nc.tensor.transpose(turned[:, t, :], state[("g", e)][:, t, half * HALF:(half + 1) * HALF], ident[:])
                rows = two.tile([P, 2, P, 2], BF16, name="x_rows_bf")
                chunk = 2 * e + half
                nc.scalar.activation(
                    rows[:], turned[:].rearrange("s (u v) p -> s u p v", v=2), COPY, scale=gate_cols[:, chunk:chunk + 1]
                )
                words = rows[:].rearrange("s u p v -> s (u p v)").bitcast(F32)
                for u in range(2):
                    nc.tensor.transpose(back[:, half, u, :], words[:, u * P:(u + 1) * P], ident[:])
            state[("back", e)] = back

        def gate_x_direct(e):
            xb = two.tile([P, C * PACK], BF16, name="x_bf", align_bytes=64)
            nc.vector.tensor_tensor(
                xb[:].rearrange("p (a i t) -> p a t i", i=4, t=PACK),
                state[("g", e)].rearrange("p t (a i) -> p a t i", i=4),
                gate_wide[:, e * C:(e + 1) * C].rearrange("p (a i) -> p a i", i=4).unsqueeze(2).to_broadcast([P, C // 4, PACK, 4]),
                MULT,
            )
            state[("xb", e)] = xb

        def words_x(e):
            xb = two.tile([P, C * PACK], BF16, name="x_bf", align_bytes=64)
            copy = nc.vector.tensor_copy if e in WORDS_ON_VECTOR else nc.scalar.copy
            copy(
                xb[:].bitcast(F32).rearrange("p (h s u) -> p h s u", h=2, u=2),
                state[("back", e)][:].rearrange("p h u s -> p h s u"),
            )
            state[("xb", e)] = xb

        def quantize(src, width, tag, pool):
            codes = pool.tile([P, width], U32, name=tag + "_codes", align_bytes=64)
            scales = pool.tile([P, width], U8, name=tag + "_scales", align_bytes=64)
            nc.vector.quantize_mx(out=codes[:].bitcast(FP8X4), scales=scales[:], in_=src)
            return codes, scales

        def quant_x(e):
            state[("xq", e)] = quantize(state[("xb", e)][:], C, "x", four)

        def cast_first(e, which):
            tag = ("w1", "w3")[which]
            if which == 0:
                state[("wb", e)] = three.tile([P, 2, PACK, P, PACK], BF16, name="w_bf", align_bytes=64)
            parts = raws[(tag, e)]
            width = P // parts
            for part in range(parts):
                cut = VECTOR_SHARE.get((e, which), 0) if parts == 1 else 0
                for copy, lo, hi in ((nc.vector.tensor_copy, 0, cut), (nc.scalar.copy, cut, width)):
                    if hi > lo:
                        copy(
                            state[("wb", e)][:, which, :, part * width + lo:part * width + hi, :].rearrange("p t m j -> p m j t"),
                            raws[(tag, e, part)][0][:].rearrange("p j (m t) -> p m j t", t=PACK)[:, lo:hi],
                        )

        def quant_first(e):
            state[("wq", e)] = quantize(state[("wb", e)][:].rearrange("p w t m j -> p (w t m j)"), 2 * H, "w", two)

        def cast_w2(g):
            wb = one.tile([P, 2, N, PACK], BF16, name="w2_bf", align_bytes=64)
            copy = nc.vector.tensor_copy if g in W2_ON_VECTOR else nc.scalar.copy
            copy(
                wb[:].rearrange("p e (a i) j -> p e a j i", i=4),
                raws[("w2", g)][:].rearrange("p e (j a i) -> p e a j i", i=4, j=PACK),
            )
            state[("w2b", g)] = wb

        def quant_w2(g):
            state[("w2q", g)] = quantize(state[("w2b", g)][:].rearrange("p e n j -> p (e n j)"), 2 * N, "w2", two)

        def product(e, which, half):
            acc = psum2.tile([P, PACK, HALF], F32, name="acc%d" % which)
            wc, ws = state[("wq", e)]
            xc, xs = state[("xq", e)]
            cols = slice(half * HALF, (half + 1) * HALF)
            for t in range(PACK):
                ch = slice(which * H + t * P, which * H + (t + 1) * P)
                nc.tensor.matmul_mx(
                    out=acc[:, t, :],
                    lhsT=wc[:, ch].bitcast(FP8X4),
                    lhsT_scale=ws[:, ch],
                    rhs=xc[:, cols].bitcast(FP8X4),
                    rhs_scale=xs[:, cols],
                    start=True,
                    stop=True,
                )
            state[("acc", which, e, half)] = acc

        def silu(e, half):
            sil = four.tile([P, HALF, PACK], F32, name="silu")
            nc.scalar.activation(sil[:], state[("acc", 0, e, half)][:].rearrange("p t s -> p s t"), SILU)
            state[("sil", e, half)] = sil

        def hidden(e, half):
            if half == 0:
                state[("hb", e)] = two.tile([P, C, PACK], BF16, name="h_bf", align_bytes=64)
            nc.vector.tensor_tensor(
                state[("hb", e)][:, half * HALF:(half + 1) * HALF, :],
                state[("acc", 1, e, half)][:].rearrange("p t s -> p s t"),
                state[("sil", e, half)][:],
                MULT,
            )

        def second(e):
            hc, hs = quantize(state[("hb", e)][:].rearrange("p s t -> p (s t)"), C, "h", two)
            wc, ws = state[("w2q", e // 2)]
            ch = slice((e % 2) * N, (e % 2 + 1) * N)
            acc = psum1.tile([P, C], F32, name="y_acc")
            nc.tensor.matmul_mx(
                out=acc[:], lhsT=wc[:, ch].bitcast(FP8X4), lhsT_scale=ws[:, ch],
                rhs=hc[:].bitcast(FP8X4), rhs_scale=hs[:], start=True, stop=True,
            )
            state[("yacc", e)] = acc

        def copy_y(e):
            nc.scalar.copy(y_sb[:, e * C:(e + 1) * C], state[("yacc", e)][:])

        load_expert(1)
        load_gate_wide(2, DIRECT)
        load_w2(0)
        for e in range(LEAD - 1):
            gather_x(e)
        for e in range(LEAD - 2):
            gate_x_direct(e)
            quant_x(e)
        for e in range(-1, E):
            nxt = e + 1 < E
            ahead = e + LEAD < E
            turn = e + LEAD - 1
            if e + 3 < E:
                load_expert(e + 3)
            if e % 2 == 0 and e + 2 < E:
                load_w2(e // 2 + 1)
            if e == 3:
                for r, pos in enumerate((pos1, pos2, pos3, pos4)):
                    nc.sync.dma_start(pos_sb[r][:], pos)
            if nxt:
                cast_first(e + 1, 0)
                cast_first(e + 1, 1)
            if e >= 0:
                silu(e, 0)
                silu(e, 1)
            if DIRECT <= turn < E:
                gate_x(turn)
            if e > 0:
                copy_y(e - 1)
            if DIRECT <= turn < E:
                words_x(turn)
            if e % 2 == 1 and nxt:
                cast_w2((e + 1) // 2)
            if nxt:
                quant_first(e + 1)
                for half in range(2):
                    product(e + 1, 0, half)
                    product(e + 1, 1, half)
            if e >= 0:
                hidden(e, 0)
                hidden(e, 1)
            if ahead:
                gather_x(e + LEAD)
            if turn < DIRECT:
                gate_x_direct(turn)
            if e >= 0:
                second(e)
            if turn < E:
                quant_x(turn)
            if e % 2 == 1 and nxt:
                quant_w2((e + 1) // 2)
        copy_y(E - 1)

        sums = {}
        for r in range(4):
            for half in range(2):
                picks = y_sb[:].indirect(pos_sb[r][:, half * 16:(half + 1) * 16])
                s = keep.tile([P, T // 2], F32, name="sum%d%d" % (r, half))
                if r == 0:
                    nc.vector.tensor_copy(s[:], picks)
                else:
                    nc.vector.tensor_tensor(s[:], picks, sums[half][:], ADD)
                sums[half] = s
                if r == 3:
                    nc.sync.dma_start(out[:, half * (T // 2):(half + 1) * (T // 2)], s[:])
